import numpy as np, ml_dtypes
CORES = [10,34,74,98]
N = 4
import mx_ref
BF = ml_dtypes.bfloat16
def entries(a):
    return np.ascontiguousarray(a.T).reshape(-1)
def table(e):
    return np.ascontiguousarray(np.reshape(e, (-1, 16)).T).astype(np.int32)
def f(rng, *shape):
    return mx_ref.flush((rng.standard_normal(shape, dtype=np.float32) * np.exp2(rng.integers(-2, 3, shape[:-1] + (1,)))).astype(BF))
def wide(rng, *shape, cols=0):
    v = rng.standard_normal(shape, dtype=np.float32) * np.exp2(rng.integers(-12, 13, shape)).astype(np.float32)
    if cols: v *= np.repeat(np.exp2(rng.integers(-cols, cols + 1, shape[:-2] + (1, shape[-1] // 4))) * (rng.random(shape[:-2] + (1, shape[-1] // 4)) > 0.0625), 4, axis=-1).astype(np.float32)
    return mx_ref.flush(v.astype(BF))
SH, CH, RD = 160, 64, 4
def lists(rng, same=False, apart=False, ends=False):
    a = []
    for r in range(N):
        p = rng.permutation(SH); e = []
        for t in range(1, RD):
            if same: c = p[:CH]
            elif apart: c = p[np.arange(CH * (t - 1), CH * t) % SH]
            elif ends: c = np.concatenate([[0, SH - 1], 1 + rng.permutation(SH - 2)[:CH - 2]])
            else: c = rng.permutation(SH)[:CH]
            e.append(rng.permutation(c))
        a.append(table(np.concatenate(e)))
    return {"idx": np.stack(a)}
def setup_inputs(rng):
    return {"wm": f(rng, N, 128, 4 * SH), "dl": f(rng, N, 128, (RD - 1) * 4 * CH), **lists(rng), "x": f(rng, N, 128, RD * 512)}
def setup_inputs_same(rng):
    return {**setup_inputs(rng), **lists(rng, same=True)}
def setup_inputs_apart(rng):
    return {**setup_inputs(rng), **lists(rng, apart=True)}
def setup_inputs_ends(rng):
    return {**setup_inputs(rng), **lists(rng, ends=True)}
def setup_inputs_big(rng):
    d = setup_inputs(rng); d["dl"] = (d["dl"].astype(np.float32) * np.float32(256)).astype(BF); return d
def setup_inputs_spread(rng):
    d = setup_inputs(rng); d["wm"] = wide(rng, N, 128, 4 * SH, cols=8); d["dl"] = wide(rng, N, 128, (RD - 1) * 4 * CH, cols=8); return d
def check_inputs(d):
    b = []
    for r in range(N):
        e = entries(d["idx"][r])
        if e.min() < 0 or e.max() >= SH: b.append("idx: range")
        for t in range(1, RD):
            if len(set(e[CH * (t - 1):CH * t].tolist())) != CH: b.append("idx: a column twice in one round")
    return b
def reference(wm, dl, idx, x):
    W = []
    for q in range(N):
        m = wm[q].reshape(128, SH, 4).copy(); d = dl[q].reshape(128, (RD - 1) * CH, 4); e = entries(idx[q])
        W.append([mx_ref.quantize(wm[q])])
        for t in range(1, RD):
            s = slice(CH * (t - 1), CH * t)
            m[:, e[s]] = (m[:, e[s]].astype(np.float32) + np.float32(0.25) * d[:, s].astype(np.float32)).astype(BF)
            W[q].append(mx_ref.quantize(m.reshape(128, 4 * SH).copy()))
    y = np.zeros((N, 128, RD * N * SH), np.float32)
    for r in range(N):
        for t in range(RD):
            X = mx_ref.quantize(np.ascontiguousarray(x[r][:, 512 * t:512 * t + 512]))
            for q in range(N):
                k = t * N + q
                y[r][:, SH * k:SH * k + SH] = mx_ref.matmul(X, W[q][t])
    return {"y": y}

@@ -1,0 +1,323 @@
+from concourse.bass import DstId, RemoteDMATransfer
+from concourse.mybir import dt, AluOpType, AxisListType, ActivationFunctionType
+
+SH, CH, RD = 160, 64, 4
+SLOT = SH + (RD - 1) * CH
+NR = 4
+NT = NR * (RD - 1)
+
+SCRATCH = {
+    "C": ("sbuf", [128, NR * SLOT], "float8_e4m3fn_x4"),
+    "CS": ("sbuf", [128, NR * SLOT], "uint8"),
+    "XB": ("sbuf", [128, RD * 512], "bfloat16"),
+    "XC": ("sbuf", [128, RD * 128], "float8_e4m3fn_x4"),
+    "XS": ("sbuf", [128, RD * 128], "uint8"),
+    "M": ("sbuf", [128, 4 * SLOT], "bfloat16"),
+    "DL": ("sbuf", [128, (RD - 1) * 4 * CH], "bfloat16"),
+    "DQ": ("sbuf", [128, (RD - 1) * 4 * CH], "bfloat16"),
+    "IDX": ("sbuf", [128, 12], "int32"),
+    "I16": ("sbuf", [128, 12], "uint16"),
+    "I4": ("sbuf", [128, 4], "uint16"),
+    "OF2": ("sbuf", [128, 4], "uint16"),
+    "OF3": ("sbuf", [128, 4], "uint16"),
+    "PT": ("sbuf", [128, 648], "float32"),
+    "VAL": ("sbuf", [128, 192], "float32"),
+    "MI": ("sbuf", [128, 64], "int32"),
+    "MJ": ("sbuf", [128, 64], "int32"),
+    "MK": ("sbuf", [128, 64], "float32"),
+    "GM2": ("sbuf", [128, 64], "float32"),
+    "GM3": ("sbuf", [128, 64], "float32"),
+    "RD2": ("sbuf", [128, 4], "float32"),
+    "RD3": ("sbuf", [128, 4], "float32"),
+    "PI": ("sbuf", [128, 1], "int32"),
+    "PA": ("sbuf", [128, 1], "int32"),
+    "PB": ("sbuf", [128, 1], "int32"),
+    "PF": ("sbuf", [128, 1], "float32"),
+    "PG": ("sbuf", [128, 1], "float32"),
+    "KB": ("sbuf", [128, 10], "float32"),
+    "LF": ("sbuf", [128, 10], "float32"),
+    "LST": ("sbuf", [128, 10], "uint16"),
+    "VP": ("sbuf", [128, 160], "float32"),
+    "VT": ("sbuf", [128, 160], "float32"),
+    "OL": ("sbuf", [128, 5], "uint16"),
+    "land": ("dram", [NR, 128, 5], "uint16"),
+    "OFF": ("sbuf", [128, NR * 40], "uint16"),
+    "R": ("sbuf", [128, NT * SLOT], "float32"),
+    "Y": ("sbuf", [128, RD * NR * SH], "float32"),
+}
+for _b in range(8):
+    SCRATCH["ps%d" % _b] = ("psum", [128, 512], "float32")
+
+SEMAPHORES = ["ldw", "ldi", "ldd", "ldx", "sv", "ss", "sp", "sg", "hc", "hs", "lsem", "own", "st"]
+SEMAPHORES += ["aw%d" % _q for _q in range(NR)] + ["ad%d" % _q for _q in range(NR)]
+SEMAPHORES += ["al%d" % _q for _q in range(NR)] + ["rp%d" % _q for _q in range(NR)]
+
+
+def helper_table(T, topo, r):
+    me = T.cores[r]
+    dests = [(r + k) % NR for k in range(1, NR)]
+    cand = {}
+    for d in dests:
+        cand[d] = [c for c in topo.cores_of(me)
+                   if topo.die(c) != topo.die(me) and T.rank_of(c) is None and topo.may_write(c, T.cores[d])]
+    out, used = {}, []
+    for d in sorted(dests, key=lambda e: len(cand[e])):
+        free = [c for c in cand[d] if c not in used]
+        free.sort(key=lambda c: sum(1 for e in dests if c in cand[e]))
+        out[d] = free[0]
+        used.append(free[0])
+    return out
+
+
+def codes(T, a, b):
+    return T.C[:, a:b].bitcast(dt.uint8)
+
+
+def helper_program(g, core, T, topo):
+    for r in range(NR):
+        for d, c in helper_table(T, topo, r).items():
+            if c != core:
+                continue
+            dst = T.cores[d]
+            m = topo.mask(core, dst)
+            rid, pid, _ = topo.addr(dst)
+            b = SLOT * r
+            n_on = len(topo.engines(T.cores[r], core))
+            g.wait_ge(T.sem.hc, n_on)
+            g.remote_dma(out_ap=codes(T, b, b + SH), in_ap=codes(T, b, b + SH), remote_sem=T.sem["aw%d" % r],
+                         local_sem=T.sem.lsem, pid=pid, routing_id=rid, dma_engine_mask=m)
+            g.wait_ge(T.sem.hs, n_on)
+            g.remote_dma(out_ap=T.CS[:, b:b + SH], in_ap=T.CS[:, b:b + SH], remote_sem=T.sem["aw%d" % r],
+                         local_sem=T.sem.lsem, pid=pid, routing_id=rid, dma_engine_mask=m)
+            g.wait_ge(T.sem.lsem, 2 * len(topo.engines(core, dst)))
+
+
+def rank_program(g, core, T, topo):
+    rank = T.rank_of(core)
+    if rank is None:
+        helper_program(g, core, T, topo)
+        return
+    add, mult = AluOpType.add, AluOpType.mult
+    Copy = ActivationFunctionType.Copy
+    eng = {"g": g, "v": g.vector, "s": g.scalar, "p": g.tensor, "y": g.sync}
+    cnt = {"sv": 0, "ss": 0, "sp": 0, "sg": 0}
+    seen = {}
+
+    def need(q, *toks):
+        for t in toks:
+            if t is not None and seen.get((q, t[0]), 0) < t[1]:
+                eng[q].wait_ge(T.sem[t[0]], t[1])
+                seen[(q, t[0])] = t[1]
+
+    def tok(sem, ins):
+        ins.then_inc(T.sem[sem], 1)
+        cnt[sem] += 1
+        return (sem, cnt[sem])
+
+    V, S = g.vector, g.scalar
+    order = [(rank - k) % NR for k in range(1, NR)]
+    dests = [(rank + k) % NR for k in range(1, NR)]
+    base = SLOT * rank
+
+    g.sync.dma_start(T.M[:, 0:4 * SH], T.wm[:]).then_inc(T.sem.ldw, 16)
+    for k in range(8):
+        e = g.scalar if k % 2 else g.sync
+        e.dma_start(T.IDX[16 * k:16 * k + 16, :], T.idx[:]).then_inc(T.sem.ldi, 16)
+    g.scalar.dma_start(T.DL[:], T.dl[:]).then_inc(T.sem.ldd, 16)
+    g.sync.dma_start(T.XB[:], T.x[:]).then_inc(T.sem.ldx, 16)
+    w_w, w_i, w_d, w_x = ("ldw", 16), ("ldi", 128), ("ldd", 16), ("ldx", 16)
+
+    t_mi = tok("sg", g.iota(T.MI[:], [[1, 64]], 128, -1))
+    t_pi = tok("sg", g.iota(T.PI[:], [[1, 1]], 0, 1))
+    t_kb = tok("sg", g.iota(T.KB[:], [[16, 5], [2, 2]], 0, 0, allow_small_or_imprecise_dtypes=True))
+    t_pt = tok("sg", g.iota(T.PT[:, 0:SH], [[1, SH]], 0, 0, allow_small_or_imprecise_dtypes=True))
+    t_va = tok("sg", g.iota(T.VAL[:], [[1, 192]], SH, 0, allow_small_or_imprecise_dtypes=True))
+    t_ms = tok("sv", V.memset(T.PT[:, 480:648], 0.0))
+    need("v", t_mi)
+    t_mj = tok("sv", V.tensor_scalar(T.MJ[:], T.MI[:], 15, None, AluOpType.bitwise_and))
+    need("v", t_pi)
+    t_pa = tok("sv", V.tensor_scalar(T.PA[:], T.PI[:], 7, None, AluOpType.bitwise_and))
+    t_pb = tok("sv", V.tensor_scalar(T.PB[:], T.PI[:], 3, None, AluOpType.arith_shift_right))
+    need("v", t_mj)
+    t_mk = tok("sv", V.tensor_scalar(T.MK[:], T.MJ[:], 0.0, 4.0, AluOpType.is_equal, mult))
+    need("v", t_pa)
+    t_pf = tok("sv", V.tensor_scalar(T.PF[:], T.PA[:], 80.0, None, mult))
+    need("v", t_pf, t_pb)
+    t_pg = tok("sv", V.tensor_tensor(T.PG[:], T.PF[:], T.PB[:], add))
+    need("v", t_pg, t_kb)
+    t_lf = tok("sv", V.tensor_scalar(T.LF[:], T.KB[:], T.PG[:, 0:1], None, add))
+    need("v", t_lf)
+    t_ls = tok("sv", V.tensor_copy(T.LST[:], T.LF[:]))
+
+    need("v", w_w)
+    t_q0 = tok("sv", V.quantize_mx(T.C[:, base:base + SH], T.CS[:, base:base + SH], T.M[:, 0:4 * SH]))
+    need("v", w_i)
+    t_i16 = tok("sv", V.tensor_copy(T.I16[:], T.IDX[:]))
+    t_i4 = tok("sv", V.tensor_scalar(T.I4[:], T.IDX[:, 0:4], 4, None, mult))
+
+    def dq(k):
+        need("s", w_d)
+        return tok("ss", S.activation(T.DQ[:, 256 * k:256 * k + 256], T.DL[:, 256 * k:256 * k + 256], Copy, scale=0.25))
+
+    def plane(k, t, off, *toks):
+        need("v", *toks)
+        a = 4 * (SH + CH * k)
+        return tok("sv", V.tensor_tensor(T.M[:, a + t:a + 4 * CH:4], T.M[:, t:a].indirect(off),
+                                         T.DQ[:, 256 * k + t:256 * k + 256:4], add))
+
+    def scatter(k, *toks):
+        need("v", *toks)
+        return tok("sv", V.tensor_copy(T.PT[:, SH * k:SH * k + SH].indirect(T.I16[:, 4 * k:4 * k + 4]),
+                                       T.VAL[:, CH * k:CH * k + CH]))
+
+    def seg(k, *toks):
+        need("s", *toks)
+        return tok("ss", S.activation(T.PT[:, SH * k:SH * k + SH], T.PT[:, SH * (k - 1):SH * k], Copy))
+
+    def look(k, gm, *toks):
+        need("v", *toks)
+        return tok("sv", V.tensor_tensor(gm[:], T.PT[:, SH * (k - 1):SH * k].indirect(T.I16[:, 4 * k:4 * k + 4]),
+                                         T.MK[:], mult))
+
+    def fold(rd, gm, *toks):
+        need("v", *toks)
+        z = None
+        for k in range(4):
+            z = tok("sv", V.tensor_reduce(rd[:, k:k + 1], gm[:, 16 * k:16 * k + 16], AxisListType.X, add))
+        return z
+
+    d1q = dq(0)
+    sc1 = scatter(0, t_i16, t_pt, t_va)
+    d1 = [plane(0, 0, T.I4[:, 0:4], t_i4, d1q, w_w)]
+    sg2 = seg(1, sc1)
+    d2q = dq(1)
+    gm2 = look(1, T.GM2, sc1, t_mk)
+    d1.append(plane(0, 1, T.I4[:, 0:4]))
+    sc2 = scatter(1, sg2)
+    sg3 = seg(2, sc2)
+    d3q = dq(2)
+    rd2 = fold(T.RD2, T.GM2, gm2)
+    gm3 = look(2, T.GM3, sc2)
+    d1.append(plane(0, 2, T.I4[:, 0:4]))
+    sc3 = scatter(2, sg3)
+    need("s", sc3, t_ms, t_ls)
+    t_vp = tok("ss", S.activation(T.VP[:], T.PT[:].indirect(T.LST[:]), Copy))
+    need("v", rd2)
+    of2 = tok("sv", V.tensor_copy(T.OF2[:], T.RD2[:]))
+    d1.append(plane(0, 3, T.I4[:, 0:4]))
+    rd3 = fold(T.RD3, T.GM3, gm3)
+    d2 = [plane(1, 0, T.OF2[:], of2, d2q, *d1)]
+    need("v", t_vp)
+    t_vt = tok("sv", V.transpose(T.VT[:], T.VP[:]))
+    d2.append(plane(1, 1, T.OF2[:]))
+    need("v", t_vt)
+    t_ol = tok("sv", V.tensor_copy(T.OL[:], T.VT[:, 0:160:32]))
+    need("v", rd3)
+    of3 = tok("sv", V.tensor_copy(T.OF3[:], T.RD3[:]))
+    d2.append(plane(1, 2, T.OF2[:]))
+    d2.append(plane(1, 3, T.OF2[:]))
+    d3 = [plane(2, 0, T.OF3[:], of3, d3q, *d2)]
+    for t in range(1, 4):
+        d3.append(plane(2, t, T.OF3[:]))
+    need("v", *d3)
+    t_qd = tok("sv", V.quantize_mx(T.C[:, base + SH:base + SLOT], T.CS[:, base + SH:base + SLOT],
+                                   T.M[:, 4 * SH:4 * SLOT]))
+    need("v", w_x)
+    t_qx = tok("sv", V.quantize_mx(T.XC[:], T.XS[:], T.XB[:]))
+
+    nl = [0]
+    ht = helper_table(T, topo, rank)
+    helpers = [ht[d] for d in dests]
+
+    def multi(dsts, out, src, sem):
+        m = topo.mask(core, dsts[0])
+        ids = []
+        for c in dsts:
+            m &= topo.mask(core, c)
+            rid, pid, _ = topo.addr(c)
+            ids.append(DstId(rid=rid, pnc=pid))
+        g.remote_dma_fused([RemoteDMATransfer(dst_ids=ids, dma_engine_mask=m, remote_sem=T.sem[sem], srcs=[src],
+                                              dsts=[out for c in dsts])], local_sem=T.sem.lsem)
+        nl[0] += len(topo.engines(core, dsts[0]))
+
+    need("g", t_q0)
+    multi(helpers, codes(T, base, base + SH), codes(T, base, base + SH), "hc")
+    multi(helpers, T.CS[:, base:base + SH], T.CS[:, base:base + SH], "hs")
+    need("g", t_ol)
+    multi([T.cores[d] for d in dests], T.land[rank], T.OL[:], "al%d" % rank)
+    need("g", t_qd)
+    for d in dests:
+        dst = T.cores[d]
+        rid, pid, _ = topo.addr(dst)
+        m = topo.mask(core, dst)
+        a, b = base + SH, base + SLOT
+        g.remote_dma(out_ap=codes(T, a, b), in_ap=codes(T, a, b), remote_sem=T.sem["ad%d" % rank],
+                     local_sem=T.sem.lsem, pid=pid, routing_id=rid, dma_engine_mask=m)
+        g.remote_dma(out_ap=T.CS[:, a:b], in_ap=T.CS[:, a:b], remote_sem=T.sem["ad%d" % rank],
+                     local_sem=T.sem.lsem, pid=pid, routing_id=rid, dma_engine_mask=m)
+        nl[0] += 2 * len(topo.engines(core, dst))
+
+    def spread(q):
+        for k in range(8):
+            g.sync.dma_start(T.OFF[16 * k:16 * k + 16, 40 * q:40 * q + 40], T.land[q]).then_inc(T.sem["rp%d" % q], 16)
+
+    need("y", t_ol)
+    g.sync.dma_start(T.land[rank], T.OL[:]).then_inc(T.sem.own, 16)
+    need("y", ("own", 16))
+    spread(rank)
+    for q in order:
+        need("y", ("al%d" % q, len(topo.engines(T.cores[q], core))))
+        spread(q)
+
+    items = [(rank, t) for t in range(RD)] + [(q, 0) for q in order] + [(q, t) for q in order for t in range(1, RD)]
+    copies, stores = [], []
+    zero_toks, nst, nr = [], [0], [0]
+    for j, (q, t) in enumerate(items):
+        n = SH + CH * t
+        bank = T["ps%d" % (j % 8)]
+        a = SLOT * q
+        need("p", t_qx)
+        if q == rank:
+            need("p", t_q0)
+            if t:
+                need("p", t_qd)
+        else:
+            hop = ht_engines(T, topo, q, core)
+            need("p", ("aw%d" % q, 2 * hop))
+            if t:
+                need("p", ("ad%d" % q, 2 * len(topo.engines(T.cores[q], core))))
+        if j >= 8:
+            need("p", copies[j - 8])
+        mm = tok("sp", g.tensor.matmul_mx(bank[:, 0:n], T.XC[:, 128 * t:128 * t + 128], T.XS[:, 128 * t:128 * t + 128],
+                                          T.C[:, a:a + n], T.CS[:, a:a + n], True, True))
+        need("s", mm)
+        blk = SH * (t * NR + q)
+        if t == 0:
+            c = tok("ss", S.activation(T.Y[:, blk:blk + SH], bank[:, 0:n], Copy))
+            copies.append(c)
+            zero_toks.append(c)
+            if len(zero_toks) == NR:
+                need("y", *zero_toks)
+                g.sync.dma_start(T.y[:, 0:NR * SH], T.Y[:, 0:NR * SH]).then_inc(T.sem.st, 16)
+                nst[0] += 16
+        else:
+            o = SLOT * nr[0]
+            nr[0] += 1
+            c = tok("ss", S.activation(T.R[:, o:o + n], bank[:, 0:n], Copy))
+            copies.append(c)
+            need("v", c, ("rp%d" % q, 128))
+            k = 40 * q + 10 * (t - 1)
+            f = tok("sv", V.tensor_copy(T.Y[:, blk:blk + SH], T.R[:, o:o + n].indirect(T.OFF[:, k:k + 10])))
+            need("y", f)
+            g.sync.dma_start(T.y[:, blk:blk + SH], T.Y[:, blk:blk + SH]).then_inc(T.sem.st, 16)
+            nst[0] += 16
+
+    need("y", ("st", nst[0]))
+    for s in ("sg", "sv", "ss", "sp"):
+        need("y", (s, cnt[s]))
+    need("g", ("lsem", nl[0]))
+
+
+def ht_engines(T, topo, q, core):
+    h = helper_table(T, topo, q)[T.rank_of(core)]
+    return len(topo.engines(h, core))

@@ -1,10 +1,13 @@
 from concourse.bass import DstId, RemoteDMATransfer
-from concourse.mybir import dt, AluOpType, AxisListType, ActivationFunctionType
+from concourse.mybir import dt, AluOpType, ActivationFunctionType
 
 SH, CH, RD = 160, 64, 4
 SLOT = SH + (RD - 1) * CH
 NR = 4
 NT = NR * (RD - 1)
+
+ROAD_W = {1: "self", 2: "self", 3: "far"}
+ROAD_D = {1: "self", 2: "self", 3: "far"}
 
 SCRATCH = {
     "C": ("sbuf", [128, NR * SLOT], "float8_e4m3fn_x4"),
@@ -18,24 +21,19 @@ SCRATCH = {
     "IDX": ("sbuf", [128, 12], "int32"),
     "I16": ("sbuf", [128, 12], "uint16"),
     "I4": ("sbuf", [128, 4], "uint16"),
-    "OF2": ("sbuf", [128, 4], "uint16"),
-    "OF3": ("sbuf", [128, 4], "uint16"),
+    "OF": ("sbuf", [128, 32], "uint16"),
     "PT": ("sbuf", [128, 648], "float32"),
     "VAL": ("sbuf", [128, 192], "float32"),
-    "MI": ("sbuf", [128, 64], "int32"),
-    "MJ": ("sbuf", [128, 64], "int32"),
+    "MI": ("sbuf", [128, 128], "int32"),
     "MK": ("sbuf", [128, 64], "float32"),
-    "GM2": ("sbuf", [128, 64], "float32"),
-    "GM3": ("sbuf", [128, 64], "float32"),
-    "RD2": ("sbuf", [128, 4], "float32"),
-    "RD3": ("sbuf", [128, 4], "float32"),
+    "RS": ("sbuf", [128, 128], "float32"),
+    "GM": ("sbuf", [128, 128], "float32"),
+    "SC": ("sbuf", [128, 128], "float32"),
     "PI": ("sbuf", [128, 1], "int32"),
-    "PA": ("sbuf", [128, 1], "int32"),
-    "PB": ("sbuf", [128, 1], "int32"),
-    "PF": ("sbuf", [128, 1], "float32"),
-    "PG": ("sbuf", [128, 1], "float32"),
+    "PA": ("sbuf", [128, 4], "int32"),
+    "PF": ("sbuf", [128, 4], "float32"),
+    "PG": ("sbuf", [128, 2], "float32"),
     "KB": ("sbuf", [128, 10], "float32"),
-    "LF": ("sbuf", [128, 10], "float32"),
     "LST": ("sbuf", [128, 10], "uint16"),
     "VP": ("sbuf", [128, 160], "float32"),
     "VT": ("sbuf", [128, 160], "float32"),
@@ -48,24 +46,24 @@ SCRATCH = {
 for _b in range(8):
     SCRATCH["ps%d" % _b] = ("psum", [128, 512], "float32")
 
-SEMAPHORES = ["ldw", "ldi", "ldd", "ldx", "sv", "ss", "sp", "sg", "hc", "hs", "lsem", "own", "st"]
+SEMAPHORES = ["ldw", "ldi", "ldd", "lde", "ldx", "sv", "ss", "sp", "sg", "hwc", "hws", "hdc", "hds", "lsem", "own", "st"]
 SEMAPHORES += ["aw%d" % _q for _q in range(NR)] + ["ad%d" % _q for _q in range(NR)]
 SEMAPHORES += ["al%d" % _q for _q in range(NR)] + ["rp%d" % _q for _q in range(NR)]
 
 
 def helper_table(T, topo, r):
     me = T.cores[r]
-    dests = [(r + k) % NR for k in range(1, NR)]
+    want = sorted(set((k, road[k]) for road in (ROAD_W, ROAD_D) for k in road if road[k] != "self"))
     cand = {}
-    for d in dests:
-        cand[d] = [c for c in topo.cores_of(me)
-                   if topo.die(c) != topo.die(me) and T.rank_of(c) is None and topo.may_write(c, T.cores[d])]
-    out, used = {}, []
-    for d in sorted(dests, key=lambda e: len(cand[e])):
-        free = [c for c in cand[d] if c not in used]
-        free.sort(key=lambda c: sum(1 for e in dests if c in cand[e]))
-        out[d] = free[0]
-        used.append(free[0])
+    for k, kind in want:
+        cand[k, kind] = [c for c in topo.cores_of(me) if T.rank_of(c) is None
+                         and (topo.die(c) == topo.die(me)) == (kind == "near")
+                         and topo.may_write(c, T.cores[(r + k) % NR])]
+    out = {}
+    for e in sorted(want, key=lambda w: len(cand[w])):
+        free = [c for c in cand[e] if c not in out.values()]
+        free.sort(key=lambda c: sum(1 for w in want if c in cand[w]))
+        out[e] = free[0]
     return out
 
 
@@ -73,23 +71,41 @@ def codes(T, a, b):
     return T.C[:, a:b].bitcast(dt.uint8)
 
 
+def bits(engines):
+    return sum(1 << e for e in engines)
+
+
+def chip_engines(T, topo, r, road):
+    me = T.cores[r]
+    on = topo.engines(me, list(helper_table(T, topo, r).values())[0])
+    if "self" not in road.values():
+        return on
+    off = topo.engines(me, T.cores[(r + 1) % NR])
+    return [e for e in on if e not in off]
+
+
 def helper_program(g, core, T, topo):
     for r in range(NR):
-        for d, c in helper_table(T, topo, r).items():
+        for (k, kind), c in helper_table(T, topo, r).items():
             if c != core:
                 continue
-            dst = T.cores[d]
-            m = topo.mask(core, dst)
-            rid, pid, _ = topo.addr(dst)
-            b = SLOT * r
-            n_on = len(topo.engines(T.cores[r], core))
-            g.wait_ge(T.sem.hc, n_on)
-            g.remote_dma(out_ap=codes(T, b, b + SH), in_ap=codes(T, b, b + SH), remote_sem=T.sem["aw%d" % r],
-                         local_sem=T.sem.lsem, pid=pid, routing_id=rid, dma_engine_mask=m)
-            g.wait_ge(T.sem.hs, n_on)
-            g.remote_dma(out_ap=T.CS[:, b:b + SH], in_ap=T.CS[:, b:b + SH], remote_sem=T.sem["aw%d" % r],
-                         local_sem=T.sem.lsem, pid=pid, routing_id=rid, dma_engine_mask=m)
-            g.wait_ge(T.sem.lsem, 2 * len(topo.engines(core, dst)))
+            q = (r + k) % NR
+            rid, pid, _ = topo.addr(T.cores[q])
+            m = topo.mask(core, T.cores[q])
+            n = 0
+            for road, a, b, got, sem in ((ROAD_W, 0, SH, "hw", "aw"), (ROAD_D, SH, SLOT, "hd", "ad")):
+                if road[k] != kind:
+                    continue
+                a, b = SLOT * r + a, SLOT * r + b
+                parts = [("c", codes(T, a, b)), ("s", T.CS[:, a:b])]
+                if list(road.values()).count("self") > 1:
+                    parts.reverse()
+                for part, view in parts:
+                    g.wait_ge(T.sem[got + part], len(chip_engines(T, topo, r, road)))
+                    g.remote_dma(out_ap=view, in_ap=view, remote_sem=T.sem[sem + str(r)], local_sem=T.sem.lsem,
+                                 pid=pid, routing_id=rid, dma_engine_mask=m)
+                    n += len(topo.engines(core, T.cores[q]))
+            g.wait_ge(T.sem.lsem, n)
 
 
 def rank_program(g, core, T, topo):
@@ -98,6 +114,7 @@ def rank_program(g, core, T, topo):
         helper_program(g, core, T, topo)
         return
     add, mult = AluOpType.add, AluOpType.mult
+    band, shr = AluOpType.bitwise_and, AluOpType.arith_shift_right
     Copy = ActivationFunctionType.Copy
     eng = {"g": g, "v": g.vector, "s": g.scalar, "p": g.tensor, "y": g.sync}
     cnt = {"sv": 0, "ss": 0, "sp": 0, "sg": 0}
@@ -115,55 +132,54 @@ def rank_program(g, core, T, topo):
         return (sem, cnt[sem])
 
     V, S = g.vector, g.scalar
-    order = [(rank - k) % NR for k in range(1, NR)]
     dests = [(rank + k) % NR for k in range(1, NR)]
     base = SLOT * rank
 
     g.sync.dma_start(T.M[:, 0:4 * SH], T.wm[:]).then_inc(T.sem.ldw, 16)
-    for k in range(8):
-        e = g.scalar if k % 2 else g.sync
+    for k in range(4):
+        e = g.scalar if k else g.sync
         e.dma_start(T.IDX[16 * k:16 * k + 16, :], T.idx[:]).then_inc(T.sem.ldi, 16)
-    g.scalar.dma_start(T.DL[:], T.dl[:]).then_inc(T.sem.ldd, 16)
-    g.sync.dma_start(T.XB[:], T.x[:]).then_inc(T.sem.ldx, 16)
-    w_w, w_i, w_d, w_x = ("ldw", 16), ("ldi", 128), ("ldd", 16), ("ldx", 16)
+    g.scalar.dma_start(T.DL[:, 0:4 * CH], T.dl[:, 0:4 * CH]).then_inc(T.sem.ldd, 16)
+    g.scalar.dma_start(T.DL[:, 4 * CH:], T.dl[:, 4 * CH:]).then_inc(T.sem.lde, 16)
+    g.scalar.dma_start(T.XB[:], T.x[:]).then_inc(T.sem.ldx, 16)
+    w_w, w_i, w_x = ("ldw", 16), ("ldi", 64), ("ldx", 16)
 
-    t_mi = tok("sg", g.iota(T.MI[:], [[1, 64]], 128, -1))
     t_pi = tok("sg", g.iota(T.PI[:], [[1, 1]], 0, 1))
+    t_mi = tok("sg", g.iota(T.MI[:], [[0, 32], [1, 4]], 0, 0))
     t_kb = tok("sg", g.iota(T.KB[:], [[16, 5], [2, 2]], 0, 0, allow_small_or_imprecise_dtypes=True))
     t_pt = tok("sg", g.iota(T.PT[:, 0:SH], [[1, SH]], 0, 0, allow_small_or_imprecise_dtypes=True))
     t_va = tok("sg", g.iota(T.VAL[:], [[1, 192]], SH, 0, allow_small_or_imprecise_dtypes=True))
     t_ms = tok("sv", V.memset(T.PT[:, 480:648], 0.0))
-    need("v", t_mi)
-    t_mj = tok("sv", V.tensor_scalar(T.MJ[:], T.MI[:], 15, None, AluOpType.bitwise_and))
     need("v", t_pi)
-    t_pa = tok("sv", V.tensor_scalar(T.PA[:], T.PI[:], 7, None, AluOpType.bitwise_and))
-    t_pb = tok("sv", V.tensor_scalar(T.PB[:], T.PI[:], 3, None, AluOpType.arith_shift_right))
-    need("v", t_mj)
-    t_mk = tok("sv", V.tensor_scalar(T.MK[:], T.MJ[:], 0.0, 4.0, AluOpType.is_equal, mult))
+    V.tensor_scalar(T.PA[:, 0:1], T.PI[:], 7, None, band)
+    V.tensor_scalar(T.PA[:, 1:2], T.PI[:], 3, None, shr)
+    V.tensor_scalar(T.PA[:, 2:3], T.PI[:], 3, None, band)
+    t_pa = tok("sv", V.tensor_scalar(T.PA[:, 3:4], T.PI[:], 2, 3, shr, band))
+    need("v", t_mi)
+    t_rs = tok("sv", V.tensor_scalar(T.RS[:], T.MI[:], 0.0, None, AluOpType.not_equal))
     need("v", t_pa)
-    t_pf = tok("sv", V.tensor_scalar(T.PF[:], T.PA[:], 80.0, None, mult))
-    need("v", t_pf, t_pb)
-    t_pg = tok("sv", V.tensor_tensor(T.PG[:], T.PF[:], T.PB[:], add))
+    t_pf = tok("sv", V.tensor_copy(T.PF[:], T.PA[:]))
+    need("v", t_pf)
+    t_mk = tok("sv", V.tensor_scalar(T.MK[:], T.MI[:, 0:CH], T.PF[:, 3:4], 4.0, AluOpType.is_equal, mult))
+    t_pg = tok("sv", V.tensor_scalar(T.PG[:, 0:1], T.PF[:, 0:1], 80.0, T.PF[:, 1:2], mult, add))
     need("v", t_pg, t_kb)
-    t_lf = tok("sv", V.tensor_scalar(T.LF[:], T.KB[:], T.PG[:, 0:1], None, add))
-    need("v", t_lf)
-    t_ls = tok("sv", V.tensor_copy(T.LST[:], T.LF[:]))
-
-    need("v", w_w)
-    t_q0 = tok("sv", V.quantize_mx(T.C[:, base:base + SH], T.CS[:, base:base + SH], T.M[:, 0:4 * SH]))
-    need("v", w_i)
-    t_i16 = tok("sv", V.tensor_copy(T.I16[:], T.IDX[:]))
-    t_i4 = tok("sv", V.tensor_scalar(T.I4[:], T.IDX[:, 0:4], 4, None, mult))
+    t_ls = tok("sv", V.tensor_scalar(T.LST[:], T.KB[:], T.PG[:, 0:1], None, add))
 
     def dq(k):
-        need("s", w_d)
+        need("s", ("lde" if k else "ldd", 16))
         return tok("ss", S.activation(T.DQ[:, 256 * k:256 * k + 256], T.DL[:, 256 * k:256 * k + 256], Copy, scale=0.25))
 
-    def plane(k, t, off, *toks):
+    def plane(t, *toks):
+        need("v", *toks)
+        a = 4 * SH
+        return tok("sv", V.tensor_tensor(T.M[:, a + t:a + 4 * CH:4], T.M[:, t:a].indirect(T.I4[:]),
+                                         T.DQ[:, t:256:4], add))
+
+    def change(k, *toks):
         need("v", *toks)
         a = 4 * (SH + CH * k)
-        return tok("sv", V.tensor_tensor(T.M[:, a + t:a + 4 * CH:4], T.M[:, t:a].indirect(off),
-                                         T.DQ[:, 256 * k + t:256 * k + 256:4], add))
+        return tok("sv", V.tensor_tensor(T.M[:, a:a + 4 * CH], T.M[:, 0:a].indirect(T.OF[:, 16 * k - 16:16 * k]),
+                                         T.DQ[:, 256 * k:256 * k + 256], add))
 
     def scatter(k, *toks):
         need("v", *toks)
@@ -174,52 +190,43 @@ def rank_program(g, core, T, topo):
         need("s", *toks)
         return tok("ss", S.activation(T.PT[:, SH * k:SH * k + SH], T.PT[:, SH * (k - 1):SH * k], Copy))
 
-    def look(k, gm, *toks):
+    def look(k, *toks):
         need("v", *toks)
-        return tok("sv", V.tensor_tensor(gm[:], T.PT[:, SH * (k - 1):SH * k].indirect(T.I16[:, 4 * k:4 * k + 4]),
-                                         T.MK[:], mult))
+        return tok("sv", V.tensor_tensor(T.GM[:, CH * k - CH:CH * k],
+                                         T.PT[:, SH * (k - 1):SH * k].indirect(T.I16[:, 4 * k:4 * k + 4]), T.MK[:], mult))
 
-    def fold(rd, gm, *toks):
-        need("v", *toks)
-        z = None
-        for k in range(4):
-            z = tok("sv", V.tensor_reduce(rd[:, k:k + 1], gm[:, 16 * k:16 * k + 16], AxisListType.X, add))
-        return z
-
+    need("v", w_w)
+    t_q0 = tok("sv", V.quantize_mx(T.C[:, base:base + SH], T.CS[:, base:base + SH], T.M[:, 0:4 * SH]))
+    need("v", w_i)
+    V.tensor_copy(T.I16[0:64, :], T.IDX[0:64, :])
+    t_i16 = tok("sv", V.tensor_copy(T.I16[64:128, :], T.IDX[0:64, :]))
     d1q = dq(0)
     sc1 = scatter(0, t_i16, t_pt, t_va)
-    d1 = [plane(0, 0, T.I4[:, 0:4], t_i4, d1q, w_w)]
     sg2 = seg(1, sc1)
-    d2q = dq(1)
-    gm2 = look(1, T.GM2, sc1, t_mk)
-    d1.append(plane(0, 1, T.I4[:, 0:4]))
+    t_i4 = tok("sv", V.tensor_scalar(T.I4[:], T.I16[:, 0:4], 4, None, mult))
+    gm2 = look(1, sc1, t_mk)
+    d1 = [plane(0, t_i4, d1q), plane(1)]
     sc2 = scatter(1, sg2)
     sg3 = seg(2, sc2)
-    d3q = dq(2)
-    rd2 = fold(T.RD2, T.GM2, gm2)
-    gm3 = look(2, T.GM3, sc2)
-    d1.append(plane(0, 2, T.I4[:, 0:4]))
+    d2q = dq(1)
+    d1.append(plane(2))
+    gm3 = look(2, sc2)
+    d1.append(plane(3))
+    need("v", gm3, t_rs)
+    t_sc = tok("sv", V.tensor_tensor_scan(T.SC[:], T.RS[:], T.GM[:], 0.0, mult, add))
     sc3 = scatter(2, sg3)
+    d3q = dq(2)
     need("s", sc3, t_ms, t_ls)
     t_vp = tok("ss", S.activation(T.VP[:], T.PT[:].indirect(T.LST[:]), Copy))
-    need("v", rd2)
-    of2 = tok("sv", V.tensor_copy(T.OF2[:], T.RD2[:]))
-    d1.append(plane(0, 3, T.I4[:, 0:4]))
-    rd3 = fold(T.RD3, T.GM3, gm3)
-    d2 = [plane(1, 0, T.OF2[:], of2, d2q, *d1)]
+    need("v", t_sc)
+    t_of = tok("sv", V.tensor_scalar(T.OF[:], T.SC[:, 3:2 * CH:4], T.PF[:, 2:3], None, add))
+    d2 = change(1, t_of, d2q, *d1)
     need("v", t_vp)
     t_vt = tok("sv", V.transpose(T.VT[:], T.VP[:]))
-    d2.append(plane(1, 1, T.OF2[:]))
+    d3 = change(2, d3q, d2)
     need("v", t_vt)
     t_ol = tok("sv", V.tensor_copy(T.OL[:], T.VT[:, 0:160:32]))
-    need("v", rd3)
-    of3 = tok("sv", V.tensor_copy(T.OF3[:], T.RD3[:]))
-    d2.append(plane(1, 2, T.OF2[:]))
-    d2.append(plane(1, 3, T.OF2[:]))
-    d3 = [plane(2, 0, T.OF3[:], of3, d3q, *d2)]
-    for t in range(1, 4):
-        d3.append(plane(2, t, T.OF3[:]))
-    need("v", *d3)
+    need("v", d3)
     t_qd = tok("sv", V.quantize_mx(T.C[:, base + SH:base + SLOT], T.CS[:, base + SH:base + SLOT],
                                    T.M[:, 4 * SH:4 * SLOT]))
     need("v", w_x)
@@ -227,97 +234,132 @@ def rank_program(g, core, T, topo):
 
     nl = [0]
     ht = helper_table(T, topo, rank)
-    helpers = [ht[d] for d in dests]
 
-    def multi(dsts, out, src, sem):
-        m = topo.mask(core, dsts[0])
-        ids = []
-        for c in dsts:
-            m &= topo.mask(core, c)
-            rid, pid, _ = topo.addr(c)
-            ids.append(DstId(rid=rid, pnc=pid))
-        g.remote_dma_fused([RemoteDMATransfer(dst_ids=ids, dma_engine_mask=m, remote_sem=T.sem[sem], srcs=[src],
-                                              dsts=[out for c in dsts])], local_sem=T.sem.lsem)
-        nl[0] += len(topo.engines(core, dsts[0]))
+    def transfer(cores, engines, view, src, sem):
+        ids = [DstId(rid=topo.addr(c)[0], pnc=topo.addr(c)[1]) for c in cores]
+        nl[0] += len(engines)
+        return RemoteDMATransfer(dst_ids=ids, dma_engine_mask=bits(engines), remote_sem=T.sem[sem], srcs=[src],
+                                 dsts=[view for c in cores])
+
+    off_chip = topo.engines(core, T.cores[dests[0]])
+
+    def send(road, a, b, got, sem):
+        views = {"c": codes(T, base + a, base + b), "s": T.CS[:, base + a:base + b]}
+        hs = [ht[k, road[k]] for k in road if road[k] != "self"]
+        ds = [T.cores[(rank + k) % NR] for k in road if road[k] == "self"]
+        if len(ds) > 1:
+            calls = [("s", hs, ds), ("c", hs, ds[:1])] + [("c", [], [d]) for d in ds[1:]]
+        else:
+            calls = [("c", hs, ds), ("s", hs, ds)]
+        for part, on, off in calls:
+            view, trs = views[part], []
+            if on:
+                trs.append(transfer(on, chip_engines(T, topo, rank, road), view, view, got + part))
+            if off:
+                trs.append(transfer(off, off_chip, view, view, sem + str(rank)))
+            g.remote_dma_fused(trs, local_sem=T.sem.lsem)
+
+    def lists():
+        need("g", t_ol)
+        g.remote_dma_fused([transfer([T.cores[d] for d in dests], off_chip, T.land[rank], T.OL[:], "al%d" % rank)],
+                           local_sem=T.sem.lsem)
 
     need("g", t_q0)
-    multi(helpers, codes(T, base, base + SH), codes(T, base, base + SH), "hc")
-    multi(helpers, T.CS[:, base:base + SH], T.CS[:, base:base + SH], "hs")
-    need("g", t_ol)
-    multi([T.cores[d] for d in dests], T.land[rank], T.OL[:], "al%d" % rank)
+    send(ROAD_W, 0, SH, "hw", "aw")
+    lists()
     need("g", t_qd)
-    for d in dests:
-        dst = T.cores[d]
-        rid, pid, _ = topo.addr(dst)
-        m = topo.mask(core, dst)
-        a, b = base + SH, base + SLOT
-        g.remote_dma(out_ap=codes(T, a, b), in_ap=codes(T, a, b), remote_sem=T.sem["ad%d" % rank],
-                     local_sem=T.sem.lsem, pid=pid, routing_id=rid, dma_engine_mask=m)
-        g.remote_dma(out_ap=T.CS[:, a:b], in_ap=T.CS[:, a:b], remote_sem=T.sem["ad%d" % rank],
-                     local_sem=T.sem.lsem, pid=pid, routing_id=rid, dma_engine_mask=m)
-        nl[0] += 2 * len(topo.engines(core, dst))
+    send(ROAD_D, SH, SLOT, "hd", "ad")
+
+    order = [(rank - k) % NR for k in range(1, NR)]
 
     def spread(q):
-        for k in range(8):
-            g.sync.dma_start(T.OFF[16 * k:16 * k + 16, 40 * q:40 * q + 40], T.land[q]).then_inc(T.sem["rp%d" % q], 16)
+        src, n = (T.OL[:], 2) if q == rank else (T.land[q], 8)
+        for k in range(n):
+            g.sync.dma_start(T.OFF[16 * k:16 * k + 16, 40 * q:40 * q + 40], src).then_inc(T.sem["rp%d" % q], 16)
+        tables[q] = ("rp%d" % q, 16 * n)
+
+    tables = {}
+
+    def repeat(q):
+        need("v", tables[q])
+        for k in range(1, 4):
+            tables[q] = tok("sv", V.tensor_copy(T.OFF[32 * k:32 * k + 32, 40 * q:40 * q + 40],
+                                                T.OFF[0:32, 40 * q:40 * q + 40]))
 
     need("y", t_ol)
-    g.sync.dma_start(T.land[rank], T.OL[:]).then_inc(T.sem.own, 16)
-    need("y", ("own", 16))
     spread(rank)
     for q in order:
-        need("y", ("al%d" % q, len(topo.engines(T.cores[q], core))))
+        need("y", ("al%d" % q, len(off_chip)))
         spread(q)
 
-    items = [(rank, t) for t in range(RD)] + [(q, 0) for q in order] + [(q, t) for q in order for t in range(1, RD)]
-    copies, stores = [], []
-    zero_toks, nst, nr = [], [0], [0]
-    for j, (q, t) in enumerate(items):
-        n = SH + CH * t
+    banks, held, nst = [], {}, [0]
+
+    def product(q, t, late, e):
+        a, n = (SH, CH * t) if late else (0, SH)
+        j = len(banks)
         bank = T["ps%d" % (j % 8)]
-        a = SLOT * q
-        need("p", t_qx)
-        if q == rank:
-            need("p", t_q0)
-            if t:
-                need("p", t_qd)
-        else:
-            hop = ht_engines(T, topo, q, core)
-            need("p", ("aw%d" % q, 2 * hop))
-            if t:
-                need("p", ("ad%d" % q, 2 * len(topo.engines(T.cores[q], core))))
+        need("p", t_qx, t_qd if q == rank else (("ad%d" if late else "aw%d") % q, 2 * len(off_chip)))
         if j >= 8:
-            need("p", copies[j - 8])
-        mm = tok("sp", g.tensor.matmul_mx(bank[:, 0:n], T.XC[:, 128 * t:128 * t + 128], T.XS[:, 128 * t:128 * t + 128],
-                                          T.C[:, a:a + n], T.CS[:, a:a + n], True, True))
-        need("s", mm)
+            need("p", banks[j - 8])
+        c, w = SLOT * q + a, max(n, 128)
+        mm = tok("sp", g.tensor.matmul_mx(bank[:, 0:w], T.XC[:, 128 * t:128 * t + 128], T.XS[:, 128 * t:128 * t + 128],
+                                          T.C[:, c:c + w], T.CS[:, c:c + w], True, True))
+        o = SLOT * (3 * q + t - 1) + a
+        out = T.R[:, o:o + n] if t else T.Y[:, SH * q:SH * q + SH]
+        need(e, mm)
+        z = tok("ss", S.activation(out, bank[:, 0:n], Copy)) if e == "s" else tok("sv", V.tensor_copy(out, bank[:, 0:n]))
+        banks.append(z)
+        held.setdefault((q, t), []).append(z)
+
+    def store(q, t, z):
         blk = SH * (t * NR + q)
-        if t == 0:
-            c = tok("ss", S.activation(T.Y[:, blk:blk + SH], bank[:, 0:n], Copy))
-            copies.append(c)
-            zero_toks.append(c)
-            if len(zero_toks) == NR:
-                need("y", *zero_toks)
-                g.sync.dma_start(T.y[:, 0:NR * SH], T.Y[:, 0:NR * SH]).then_inc(T.sem.st, 16)
-                nst[0] += 16
-        else:
-            o = SLOT * nr[0]
-            nr[0] += 1
-            c = tok("ss", S.activation(T.R[:, o:o + n], bank[:, 0:n], Copy))
-            copies.append(c)
-            need("v", c, ("rp%d" % q, 128))
-            k = 40 * q + 10 * (t - 1)
-            f = tok("sv", V.tensor_copy(T.Y[:, blk:blk + SH], T.R[:, o:o + n].indirect(T.OFF[:, k:k + 10])))
-            need("y", f)
-            g.sync.dma_start(T.y[:, blk:blk + SH], T.Y[:, blk:blk + SH]).then_inc(T.sem.st, 16)
-            nst[0] += 16
+        need("y", z)
+        g.sync.dma_start(T.y[:, blk:blk + SH], T.Y[:, blk:blk + SH]).then_inc(T.sem.st, 16)
+        nst[0] += 16
+
+    def pick(q, t, e):
+        need(e, tables[q], *held[q, t])
+        o, k, blk = SLOT * (3 * q + t - 1), 40 * q + 10 * (t - 1), SH * (t * NR + q)
+        win = T.R[:, o:o + SH + CH * t].indirect(T.OFF[:, k:k + 10])
+        out = T.Y[:, blk:blk + SH]
+        store(q, t, tok("ss", S.activation(out, win, Copy)) if e == "s" else tok("sv", V.tensor_copy(out, win)))
+
+    load = {"v": 0, "s": 0}
+
+    def lighter(n):
+        e = "v" if load["v"] <= load["s"] else "s"
+        load[e] += n + 64
+        return e
+
+    def early(q):
+        for t in range(RD):
+            product(q, t, False, lighter(SH))
+        store(q, 0, held[q, 0][0])
+
+    def late(q):
+        for t in range(RD - 1, 0, -1):
+            product(q, t, True, lighter(CH * t))
+
+    def picks(q):
+        for t in range(1, RD):
+            pick(q, t, lighter(3 * SH // 2))
+
+    first, second, far = order
+    early(rank)
+    late(rank)
+    repeat(rank)
+    early(first)
+    picks(rank)
+    early(second)
+    late(first)
+    picks(first)
+    early(far)
+    late(second)
+    picks(second)
+    late(far)
+    picks(far)
 
     need("y", ("st", nst[0]))
     for s in ("sg", "sv", "ss", "sp"):
         need("y", (s, cnt[s]))
     need("g", ("lsem", nl[0]))
-
-
-def ht_engines(T, topo, q, core):
-    h = helper_table(T, topo, q)[T.rank_of(core)]
-    return len(topo.engines(h, core))

@@ -5,9 +5,17 @@ SH, CH, RD = 160, 64, 4
 SLOT = SH + (RD - 1) * CH
 NR = 4
 NT = NR * (RD - 1)
+GATE = 0
+QUEUE = "svvs"
+NSP = (2, 2)
+XE = 0
+CHAIN = "i16 sc1 seg2 mk ls q0 i4 look2 dq1 sc2 seg3 look3 p0 p1 scan sc3 dq2 vp dq3 of p2 p3 d2 vt xa d3 ol qd xb"
 
-ROAD_W = {1: "self", 2: "self", 3: "far"}
-ROAD_D = {1: "self", 2: "self", 3: "far"}
+PIECES = {"w": (0, SH), "d": (SH, SLOT)}
+CALLS = [("ws", "b", [1]), ("wc", "a", [1]), ("wc", "", [2]), ("lists", "", []),
+         ("ds", "b", [1]), ("dc", "a", [1]), ("dc0", "", [2])]
+HELPERS = {"a": ("far", [("wc", [3]), ("dc1", [2]), ("dc", [3])]),
+           "b": ("far", [("ws", [2, 3]), ("ds", [2, 3])])}
 
 SCRATCH = {
     "C": ("sbuf", [128, NR * SLOT], "float8_e4m3fn_x4"),
@@ -22,9 +30,8 @@ SCRATCH = {
     "I16": ("sbuf", [128, 12], "uint16"),
     "I4": ("sbuf", [128, 4], "uint16"),
     "OF": ("sbuf", [128, 32], "uint16"),
-    "PT": ("sbuf", [128, 648], "float32"),
-    "VAL": ("sbuf", [128, 192], "float32"),
-    "MI": ("sbuf", [128, 128], "int32"),
+    "PT": ("sbuf", [128, 2 * SH + SLOT], "float32"),
+    "MI": ("sbuf", [128, 64], "int32"),
     "MK": ("sbuf", [128, 64], "float32"),
     "RS": ("sbuf", [128, 128], "float32"),
     "GM": ("sbuf", [128, 128], "float32"),
@@ -46,24 +53,23 @@ SCRATCH = {
 for _b in range(8):
     SCRATCH["ps%d" % _b] = ("psum", [128, 512], "float32")
 
-SEMAPHORES = ["ldw", "ldi", "ldd", "lde", "ldx", "sv", "ss", "sp", "sg", "hwc", "hws", "hdc", "hds", "lsem", "own", "st"]
+SEMAPHORES = ["ldw", "ldi", "ldd", "lde", "ldx", "ldy", "sv", "ss", "sp", "sg", "hwc", "hws", "hdc", "hds", "lsem", "own", "st"]
 SEMAPHORES += ["aw%d" % _q for _q in range(NR)] + ["ad%d" % _q for _q in range(NR)]
 SEMAPHORES += ["al%d" % _q for _q in range(NR)] + ["rp%d" % _q for _q in range(NR)]
 
 
 def helper_table(T, topo, r):
     me = T.cores[r]
-    want = sorted(set((k, road[k]) for road in (ROAD_W, ROAD_D) for k in road if road[k] != "self"))
     cand = {}
-    for k, kind in want:
-        cand[k, kind] = [c for c in topo.cores_of(me) if T.rank_of(c) is None
-                         and (topo.die(c) == topo.die(me)) == (kind == "near")
-                         and topo.may_write(c, T.cores[(r + k) % NR])]
+    for h, (kind, jobs) in HELPERS.items():
+        cand[h] = [c for c in topo.cores_of(me) if T.rank_of(c) is None
+                   and (topo.die(c) == topo.die(me)) == (kind == "near")
+                   and all(topo.may_write(c, T.cores[(r + k) % NR]) for _, ks in jobs for k in ks)]
     out = {}
-    for e in sorted(want, key=lambda w: len(cand[w])):
-        free = [c for c in cand[e] if c not in out.values()]
-        free.sort(key=lambda c: sum(1 for w in want if c in cand[w]))
-        out[e] = free[0]
+    for h in sorted(cand, key=lambda e: len(cand[e])):
+        free = [c for c in cand[h] if c not in out.values()]
+        free.sort(key=lambda c: sum(1 for e in cand if c in cand[e]))
+        out[h] = free[0]
     return out
 
 
@@ -75,36 +81,43 @@ def bits(engines):
     return sum(1 << e for e in engines)
 
 
-def chip_engines(T, topo, r, road):
+def chip_engines(T, topo, r):
     me = T.cores[r]
-    on = topo.engines(me, list(helper_table(T, topo, r).values())[0])
-    if "self" not in road.values():
-        return on
     off = topo.engines(me, T.cores[(r + 1) % NR])
-    return [e for e in on if e not in off]
+    return [e for e in topo.engines(me, list(helper_table(T, topo, r).values())[0]) if e not in off]
+
+
+def view(T, r, what):
+    a, b = PIECES[what[0]]
+    if what[2:]:
+        a, b = ((a, (a + b) // 2), ((a + b) // 2, b))[int(what[2])]
+    return codes(T, SLOT * r + a, SLOT * r + b) if what[1] == "c" else T.CS[:, SLOT * r + a:SLOT * r + b]
+
+
+def writes(piece, k):
+    jobs = [(what, ks) for what, _, ks in CALLS] + [j for h in HELPERS for j in HELPERS[h][1]]
+    return sum(1 for what, ks in jobs if what[0] == piece and k in ks)
+
+
+def transfer(T, topo, cores, engines, out, src, sem):
+    ids = [DstId(rid=topo.addr(c)[0], pnc=topo.addr(c)[1]) for c in cores]
+    return RemoteDMATransfer(dst_ids=ids, dma_engine_mask=bits(engines), remote_sem=T.sem[sem], srcs=[src],
+                             dsts=[out for c in cores])
 
 
 def helper_program(g, core, T, topo):
     for r in range(NR):
-        for (k, kind), c in helper_table(T, topo, r).items():
+        for h, c in helper_table(T, topo, r).items():
             if c != core:
                 continue
-            q = (r + k) % NR
-            rid, pid, _ = topo.addr(T.cores[q])
-            m = topo.mask(core, T.cores[q])
             n = 0
-            for road, a, b, got, sem in ((ROAD_W, 0, SH, "hw", "aw"), (ROAD_D, SH, SLOT, "hd", "ad")):
-                if road[k] != kind:
-                    continue
-                a, b = SLOT * r + a, SLOT * r + b
-                parts = [("c", codes(T, a, b)), ("s", T.CS[:, a:b])]
-                if list(road.values()).count("self") > 1:
-                    parts.reverse()
-                for part, view in parts:
-                    g.wait_ge(T.sem[got + part], len(chip_engines(T, topo, r, road)))
-                    g.remote_dma(out_ap=view, in_ap=view, remote_sem=T.sem[sem + str(r)], local_sem=T.sem.lsem,
-                                 pid=pid, routing_id=rid, dma_engine_mask=m)
-                    n += len(topo.engines(core, T.cores[q]))
+            for what, ks in HELPERS[h][1]:
+                cores = [T.cores[(r + k) % NR] for k in ks]
+                engines = topo.engines(core, cores[0])
+                g.wait_ge(T.sem["h" + what[0:2]], len(chip_engines(T, topo, r)))
+                g.remote_dma_fused([transfer(T, topo, cores, engines, view(T, r, what), view(T, r, what),
+                                             "a%s%d" % (what[0], r))], local_sem=T.sem.lsem)
+                n += len(engines)
             g.wait_ge(T.sem.lsem, n)
 
 
@@ -135,35 +148,33 @@ def rank_program(g, core, T, topo):
     dests = [(rank + k) % NR for k in range(1, NR)]
     base = SLOT * rank
 
-    g.sync.dma_start(T.M[:, 0:4 * SH], T.wm[:]).then_inc(T.sem.ldw, 16)
-    for k in range(4):
-        e = g.scalar if k else g.sync
+    for k in range(2):
+        e = g.scalar if k % 2 else g.sync
         e.dma_start(T.IDX[16 * k:16 * k + 16, :], T.idx[:]).then_inc(T.sem.ldi, 16)
-    g.scalar.dma_start(T.DL[:, 0:4 * CH], T.dl[:, 0:4 * CH]).then_inc(T.sem.ldd, 16)
-    g.scalar.dma_start(T.DL[:, 4 * CH:], T.dl[:, 4 * CH:]).then_inc(T.sem.lde, 16)
-    g.scalar.dma_start(T.XB[:], T.x[:]).then_inc(T.sem.ldx, 16)
-    w_w, w_i, w_x = ("ldw", 16), ("ldi", 64), ("ldx", 16)
+    g.sync.dma_start(T.M[:, 0:4 * SH], T.wm[:]).then_inc(T.sem.ldw, 16)
+    g.sync.dma_start(T.DL[:, 0:4 * CH], T.dl[:, 0:4 * CH]).then_inc(T.sem.ldd, 16)
+    g.sync.dma_start(T.DL[:, 4 * CH:], T.dl[:, 4 * CH:]).then_inc(T.sem.lde, 16)
+    if XE:
+        g.sync.dma_start(T.XB[:, 0:512 * XE], T.x[:, 0:512 * XE]).then_inc(T.sem.ldy, 16)
+    g.sync.dma_start(T.XB[:, 512 * XE:], T.x[:, 512 * XE:]).then_inc(T.sem.ldx, 16)
+    w_w, w_i = ("ldw", 16), ("ldi", 32)
 
     t_pi = tok("sg", g.iota(T.PI[:], [[1, 1]], 0, 1))
-    t_mi = tok("sg", g.iota(T.MI[:], [[0, 32], [1, 4]], 0, 0))
+    t_pt = tok("sg", g.iota(T.PT[:, 2 * SH:], [[1, SLOT]], 0, 0, allow_small_or_imprecise_dtypes=True))
+    t_mi = tok("sg", g.iota(T.MI[:], [[0, 16], [1, 4]], 0, 0))
     t_kb = tok("sg", g.iota(T.KB[:], [[16, 5], [2, 2]], 0, 0, allow_small_or_imprecise_dtypes=True))
-    t_pt = tok("sg", g.iota(T.PT[:, 0:SH], [[1, SH]], 0, 0, allow_small_or_imprecise_dtypes=True))
-    t_va = tok("sg", g.iota(T.VAL[:], [[1, 192]], SH, 0, allow_small_or_imprecise_dtypes=True))
-    t_ms = tok("sv", V.memset(T.PT[:, 480:648], 0.0))
+    t_r1 = tok("sv", V.memset(T.RS[:], 1.0))
     need("v", t_pi)
     V.tensor_scalar(T.PA[:, 0:1], T.PI[:], 7, None, band)
     V.tensor_scalar(T.PA[:, 1:2], T.PI[:], 3, None, shr)
     V.tensor_scalar(T.PA[:, 2:3], T.PI[:], 3, None, band)
     t_pa = tok("sv", V.tensor_scalar(T.PA[:, 3:4], T.PI[:], 2, 3, shr, band))
-    need("v", t_mi)
-    t_rs = tok("sv", V.tensor_scalar(T.RS[:], T.MI[:], 0.0, None, AluOpType.not_equal))
+    need("v", t_r1)
+    t_rs = tok("sv", V.memset(T.RS[:, 0:2 * CH:4], 0.0))
     need("v", t_pa)
     t_pf = tok("sv", V.tensor_copy(T.PF[:], T.PA[:]))
     need("v", t_pf)
-    t_mk = tok("sv", V.tensor_scalar(T.MK[:], T.MI[:, 0:CH], T.PF[:, 3:4], 4.0, AluOpType.is_equal, mult))
     t_pg = tok("sv", V.tensor_scalar(T.PG[:, 0:1], T.PF[:, 0:1], 80.0, T.PF[:, 1:2], mult, add))
-    need("v", t_pg, t_kb)
-    t_ls = tok("sv", V.tensor_scalar(T.LST[:], T.KB[:], T.PG[:, 0:1], None, add))
 
     def dq(k):
         need("s", ("lde" if k else "ldd", 16))
@@ -181,124 +192,134 @@ def rank_program(g, core, T, topo):
         return tok("sv", V.tensor_tensor(T.M[:, a:a + 4 * CH], T.M[:, 0:a].indirect(T.OF[:, 16 * k - 16:16 * k]),
                                          T.DQ[:, 256 * k:256 * k + 256], add))
 
+    def table(t):
+        return T.PT[:, SH * (3 - t):SH * (4 - t)]
+
     def scatter(k, *toks):
         need("v", *toks)
-        return tok("sv", V.tensor_copy(T.PT[:, SH * k:SH * k + SH].indirect(T.I16[:, 4 * k:4 * k + 4]),
-                                       T.VAL[:, CH * k:CH * k + CH]))
+        a = 3 * SH + CH * k
+        return tok("sv", V.tensor_copy(table(k + 1).indirect(T.I16[:, 4 * k:4 * k + 4]), T.PT[:, a:a + CH]))
 
     def seg(k, *toks):
         need("s", *toks)
-        return tok("ss", S.activation(T.PT[:, SH * k:SH * k + SH], T.PT[:, SH * (k - 1):SH * k], Copy))
+        return tok("ss", S.activation(table(k + 1), table(k), Copy))
 
     def look(k, *toks):
         need("v", *toks)
         return tok("sv", V.tensor_tensor(T.GM[:, CH * k - CH:CH * k],
-                                         T.PT[:, SH * (k - 1):SH * k].indirect(T.I16[:, 4 * k:4 * k + 4]), T.MK[:], mult))
+                                         table(k).indirect(T.I16[:, 4 * k:4 * k + 4]), T.MK[:], mult))
 
-    need("v", w_w)
-    t_q0 = tok("sv", V.quantize_mx(T.C[:, base:base + SH], T.CS[:, base:base + SH], T.M[:, 0:4 * SH]))
-    need("v", w_i)
-    V.tensor_copy(T.I16[0:64, :], T.IDX[0:64, :])
-    t_i16 = tok("sv", V.tensor_copy(T.I16[64:128, :], T.IDX[0:64, :]))
-    d1q = dq(0)
-    sc1 = scatter(0, t_i16, t_pt, t_va)
-    sg2 = seg(1, sc1)
-    t_i4 = tok("sv", V.tensor_scalar(T.I4[:], T.I16[:, 0:4], 4, None, mult))
-    gm2 = look(1, sc1, t_mk)
-    d1 = [plane(0, t_i4, d1q), plane(1)]
-    sc2 = scatter(1, sg2)
-    sg3 = seg(2, sc2)
-    d2q = dq(1)
-    d1.append(plane(2))
-    gm3 = look(2, sc2)
-    d1.append(plane(3))
-    need("v", gm3, t_rs)
-    t_sc = tok("sv", V.tensor_tensor_scan(T.SC[:], T.RS[:], T.GM[:], 0.0, mult, add))
-    sc3 = scatter(2, sg3)
-    d3q = dq(2)
-    need("s", sc3, t_ms, t_ls)
-    t_vp = tok("ss", S.activation(T.VP[:], T.PT[:].indirect(T.LST[:]), Copy))
-    need("v", t_sc)
-    t_of = tok("sv", V.tensor_scalar(T.OF[:], T.SC[:, 3:2 * CH:4], T.PF[:, 2:3], None, add))
-    d2 = change(1, t_of, d2q, *d1)
-    need("v", t_vp)
-    t_vt = tok("sv", V.transpose(T.VT[:], T.VP[:]))
-    d3 = change(2, d3q, d2)
-    need("v", t_vt)
-    t_ol = tok("sv", V.tensor_copy(T.OL[:], T.VT[:, 0:160:32]))
-    need("v", d3)
-    t_qd = tok("sv", V.quantize_mx(T.C[:, base + SH:base + SLOT], T.CS[:, base + SH:base + SLOT],
-                                   T.M[:, 4 * SH:4 * SLOT]))
-    need("v", w_x)
-    t_qx = tok("sv", V.quantize_mx(T.XC[:], T.XS[:], T.XB[:]))
+    t_qx = {}
+
+    def quant_x(a, b):
+        if a < b:
+            need("v", ("ldx" if b > XE else "ldy", 16))
+            z = tok("sv", V.quantize_mx(T.XC[:, 128 * a:128 * b], T.XS[:, 128 * a:128 * b], T.XB[:, 512 * a:512 * b]))
+            t_qx.update({t: z for t in range(a, b)})
+
+    def quant(a, b, *toks):
+        need("v", *toks)
+        return tok("sv", V.quantize_mx(T.C[:, base + a:base + b], T.CS[:, base + a:base + b], T.M[:, 4 * a:4 * b]))
+
+    def on(q, toks, call):
+        need(q, *toks)
+        return tok("s" + q, call())
+
+    def narrow():
+        need("v", w_i)
+        for k in range(0, 96, 32):
+            V.tensor_copy(T.I16[k:k + 32, :], T.IDX[0:32, :])
+        return tok("sv", V.tensor_copy(T.I16[96:128, :], T.IDX[0:32, :]))
+
+    z = {}
+    steps = {
+        "q0": lambda: quant(0, SH, w_w),
+        "i16": narrow,
+        "mk": lambda: on("v", [t_pf, t_mi],
+                         lambda: V.tensor_scalar(T.MK[:], T.MI[:], T.PF[:, 3:4], 4.0, AluOpType.is_equal, mult)),
+        "ls": lambda: on("v", [t_pg, t_kb], lambda: V.tensor_scalar(T.LST[:], T.KB[:], T.PG[:, 0:1], None, add)),
+        "i4": lambda: on("v", [z["i16"]], lambda: V.tensor_scalar(T.I4[:], T.I16[:, 0:4], 4, None, mult)),
+        "dq1": lambda: dq(0), "dq2": lambda: dq(1), "dq3": lambda: dq(2),
+        "sc1": lambda: scatter(0, z["i16"], t_pt),
+        "sc2": lambda: scatter(1, z["seg2"]),
+        "sc3": lambda: scatter(2, z["seg3"]),
+        "seg2": lambda: seg(1, z["sc1"]),
+        "seg3": lambda: seg(2, z["sc2"]),
+        "look2": lambda: look(1, z["sc1"], z["mk"]),
+        "look3": lambda: look(2, z["sc2"], z["mk"]),
+        "p0": lambda: plane(0, z["i4"], z["dq1"], w_w),
+        "p1": lambda: plane(1), "p2": lambda: plane(2), "p3": lambda: plane(3),
+        "scan": lambda: on("v", [z["look2"], z["look3"], t_rs],
+                           lambda: V.tensor_tensor_scan(T.SC[:], T.RS[:], T.GM[:], 0.0, mult, add)),
+        "of": lambda: on("v", [z["scan"]],
+                         lambda: V.tensor_scalar(T.OF[:], T.SC[:, 3:2 * CH:4], T.PF[:, 2:3], None, add)),
+        "d2": lambda: change(1, z["of"], z["dq2"], z["p3"]),
+        "d3": lambda: change(2, z["dq3"], z["d2"]),
+        "vp": lambda: on("s", [z["sc3"], z["ls"]],
+                         lambda: S.activation(T.VP[:], T.PT[:].indirect(T.LST[:]), Copy)),
+        "vt": lambda: on("v", [z["vp"]], lambda: V.transpose(T.VT[:], T.VP[:])),
+        "ol": lambda: on("v", [z["vt"]], lambda: V.tensor_copy(T.OL[:], T.VT[:, 0:160:32])),
+        "qd": lambda: quant(SH, SLOT, z["d3"]),
+        "xa": lambda: quant_x(0, XE), "xb": lambda: quant_x(XE, RD),
+    }
+    for name in CHAIN.split():
+        z[name] = steps[name]()
+    t_q0, t_qd, t_ol = z["q0"], z["qd"], z["ol"]
 
     nl = [0]
     ht = helper_table(T, topo, rank)
 
-    def transfer(cores, engines, view, src, sem):
-        ids = [DstId(rid=topo.addr(c)[0], pnc=topo.addr(c)[1]) for c in cores]
-        nl[0] += len(engines)
-        return RemoteDMATransfer(dst_ids=ids, dma_engine_mask=bits(engines), remote_sem=T.sem[sem], srcs=[src],
-                                 dsts=[view for c in cores])
-
     off_chip = topo.engines(core, T.cores[dests[0]])
-
-    def send(road, a, b, got, sem):
-        views = {"c": codes(T, base + a, base + b), "s": T.CS[:, base + a:base + b]}
-        hs = [ht[k, road[k]] for k in road if road[k] != "self"]
-        ds = [T.cores[(rank + k) % NR] for k in road if road[k] == "self"]
-        if len(ds) > 1:
-            calls = [("s", hs, ds), ("c", hs, ds[:1])] + [("c", [], [d]) for d in ds[1:]]
-        else:
-            calls = [("c", hs, ds), ("s", hs, ds)]
-        for part, on, off in calls:
-            view, trs = views[part], []
-            if on:
-                trs.append(transfer(on, chip_engines(T, topo, rank, road), view, view, got + part))
-            if off:
-                trs.append(transfer(off, off_chip, view, view, sem + str(rank)))
-            g.remote_dma_fused(trs, local_sem=T.sem.lsem)
-
-    def lists():
-        need("g", t_ol)
-        g.remote_dma_fused([transfer([T.cores[d] for d in dests], off_chip, T.land[rank], T.OL[:], "al%d" % rank)],
-                           local_sem=T.sem.lsem)
-
-    need("g", t_q0)
-    send(ROAD_W, 0, SH, "hw", "aw")
-    lists()
-    need("g", t_qd)
-    send(ROAD_D, SH, SLOT, "hd", "ad")
+    on_chip = chip_engines(T, topo, rank)
+    made = {"w": t_q0, "d": t_qd, "l": t_ol}
+    for what, hs, ks in CALLS:
+        need("g", made[what[0]])
+        if GATE and (what, hs, ks) == CALLS[-1]:
+            need("g", ("own", 1))
+        trs = []
+        if what == "lists":
+            trs.append(transfer(T, topo, [T.cores[d] for d in dests], off_chip, T.land[rank], T.OL[:], "al%d" % rank))
+        if hs:
+            v = view(T, rank, what)
+            trs.append(transfer(T, topo, [ht[h] for h in hs], on_chip, v, v, "h" + what[0:2]))
+        if ks:
+            v = view(T, rank, what)
+            trs.append(transfer(T, topo, [T.cores[(rank + k) % NR] for k in ks], off_chip, v, v,
+                                "a%s%d" % (what[0], rank)))
+        g.remote_dma_fused(trs, local_sem=T.sem.lsem)
+        nl[0] += len(on_chip) * bool(hs) + len(off_chip) * (len(trs) - bool(hs))
 
     order = [(rank - k) % NR for k in range(1, NR)]
 
     def spread(q):
-        src, n = (T.OL[:], 2) if q == rank else (T.land[q], 8)
+        need("y", t_ol if q == rank else ("al%d" % q, len(off_chip)))
+        src, a = T.OL[:] if q == rank else T.land[q], 40 * ((rank - q) % NR)
+        n = NSP[q != rank]
         for k in range(n):
-            g.sync.dma_start(T.OFF[16 * k:16 * k + 16, 40 * q:40 * q + 40], src).then_inc(T.sem["rp%d" % q], 16)
+            g.sync.dma_start(T.OFF[16 * k:16 * k + 16, a:a + 40], src).then_inc(T.sem["rp%d" % q], 16)
         tables[q] = ("rp%d" % q, 16 * n)
+        if GATE and len(tables) == NR:
+            g.sync.sem_inc(T.sem.own, 1)
 
     tables = {}
 
-    def repeat(q):
-        need("v", tables[q])
-        for k in range(1, 4):
-            tables[q] = tok("sv", V.tensor_copy(T.OFF[32 * k:32 * k + 32, 40 * q:40 * q + 40],
-                                                T.OFF[0:32, 40 * q:40 * q + 40]))
-
-    need("y", t_ol)
-    spread(rank)
-    for q in order:
-        need("y", ("al%d" % q, len(off_chip)))
-        spread(q)
+    def repeat(*qs):
+        need("v", *[tables[q] for q in qs])
+        a, b = 40 * ((rank - qs[0]) % NR), 40 * ((rank - qs[-1]) % NR + 1)
+        n = 16 * NSP[qs[0] != rank]
+        for k in range(n, 128, n):
+            z = tok("sv", V.tensor_copy(T.OFF[k:k + n, a:b], T.OFF[0:n, a:b]))
+            tables.update({q: z for q in qs})
 
     banks, held, nst = [], {}, [0]
 
-    def product(q, t, late, e):
-        a, n = (SH, CH * t) if late else (0, SH)
+    def product(q, t, parts, e):
+        a = 0 if "w" in parts else SH
+        n = (SH + CH * t if "d" in parts else SH) - a
         j = len(banks)
         bank = T["ps%d" % (j % 8)]
-        need("p", t_qx, t_qd if q == rank else (("ad%d" if late else "aw%d") % q, 2 * len(off_chip)))
+        need("p", t_qx[t], *[made[p] if q == rank else ("a%s%d" % (p, q), writes(p, (rank - q) % NR) * len(off_chip))
+                             for p in parts])
         if j >= 8:
             need("p", banks[j - 8])
         c, w = SLOT * q + a, max(n, 128)
@@ -311,49 +332,59 @@ def rank_program(g, core, T, topo):
         banks.append(z)
         held.setdefault((q, t), []).append(z)
 
+    ready = {}
+
     def store(q, t, z):
-        blk = SH * (t * NR + q)
-        need("y", z)
-        g.sync.dma_start(T.y[:, blk:blk + SH], T.Y[:, blk:blk + SH]).then_inc(T.sem.st, 16)
-        nst[0] += 16
+        ready[t * NR + q] = z
+
+    def flush():
+        while ready:
+            a = b = min(ready)
+            while b in ready:
+                need("y", ready.pop(b))
+                b += 1
+            g.sync.dma_start(T.y[:, SH * a:SH * b], T.Y[:, SH * a:SH * b]).then_inc(T.sem.st, 16)
+            nst[0] += 16
 
     def pick(q, t, e):
         need(e, tables[q], *held[q, t])
-        o, k, blk = SLOT * (3 * q + t - 1), 40 * q + 10 * (t - 1), SH * (t * NR + q)
+        o, k, blk = SLOT * (3 * q + t - 1), 40 * ((rank - q) % NR) + 10 * (3 - t), SH * (t * NR + q)
         win = T.R[:, o:o + SH + CH * t].indirect(T.OFF[:, k:k + 10])
         out = T.Y[:, blk:blk + SH]
         store(q, t, tok("ss", S.activation(out, win, Copy)) if e == "s" else tok("sv", V.tensor_copy(out, win)))
 
-    load = {"v": 0, "s": 0}
+    def early(q, ts=(1, 3, 2, 0), e=None):
+        for t in ts:
+            product(q, t, "w", e or QUEUE[t])
+            if t == 0:
+                store(q, 0, held[q, 0][0])
 
-    def lighter(n):
-        e = "v" if load["v"] <= load["s"] else "s"
-        load[e] += n + 64
-        return e
+    def late(q, ts=(1, 3, 2), e=None):
+        for t in ts:
+            product(q, t, "wd" if (q, t) not in held else "d", e or QUEUE[t])
 
-    def early(q):
-        for t in range(RD):
-            product(q, t, False, lighter(SH))
-        store(q, 0, held[q, 0][0])
-
-    def late(q):
-        for t in range(RD - 1, 0, -1):
-            product(q, t, True, lighter(CH * t))
-
-    def picks(q):
-        for t in range(1, RD):
-            pick(q, t, lighter(3 * SH // 2))
+    def picks(*qs):
+        for t in (1, 3, 2):
+            for q in qs:
+                pick(q, t, QUEUE[t])
+            flush()
 
     first, second, far = order
-    early(rank)
+    spread(rank)
+    for q in order:
+        spread(q)
+    early(rank, [0])
+    flush()
     late(rank)
     repeat(rank)
     early(first)
     picks(rank)
     early(second)
+    early(far)
+    flush()
+    repeat(*order)
     late(first)
     picks(first)
-    early(far)
     late(second)
     picks(second)
     late(far)

from concourse.bass import DstId, RemoteDMATransfer
from concourse.mybir import dt, AluOpType, ActivationFunctionType

SH, CH, RD = 160, 64, 4
SLOT = SH + (RD - 1) * CH
NR = 4
NT = NR * (RD - 1)
GATE = 0
QUEUE = "svvs"
NSP = (2, 2)
XE = 0
CHAIN = "i16 sc1 seg2 mk ls q0 i4 look2 dq1 sc2 seg3 look3 p0 p1 scan sc3 dq2 vp dq3 of p2 p3 d2 vt xa d3 ol qd xb"

PIECES = {"w": (0, SH), "d": (SH, SLOT)}
CALLS = [("ws", "b", [1]), ("wc", "a", [1]), ("wc", "", [2]), ("lists", "", []),
         ("ds", "b", [1]), ("dc", "a", [1]), ("dc0", "", [2])]
HELPERS = {"a": ("far", [("wc", [3]), ("dc1", [2]), ("dc", [3])]),
           "b": ("far", [("ws", [2, 3]), ("ds", [2, 3])])}

SCRATCH = {
    "C": ("sbuf", [128, NR * SLOT], "float8_e4m3fn_x4"),
    "CS": ("sbuf", [128, NR * SLOT], "uint8"),
    "XB": ("sbuf", [128, RD * 512], "bfloat16"),
    "XC": ("sbuf", [128, RD * 128], "float8_e4m3fn_x4"),
    "XS": ("sbuf", [128, RD * 128], "uint8"),
    "M": ("sbuf", [128, 4 * SLOT], "bfloat16"),
    "DL": ("sbuf", [128, (RD - 1) * 4 * CH], "bfloat16"),
    "DQ": ("sbuf", [128, (RD - 1) * 4 * CH], "bfloat16"),
    "IDX": ("sbuf", [128, 12], "int32"),
    "I16": ("sbuf", [128, 12], "uint16"),
    "I4": ("sbuf", [128, 4], "uint16"),
    "OF": ("sbuf", [128, 32], "uint16"),
    "PT": ("sbuf", [128, 2 * SH + SLOT], "float32"),
    "MI": ("sbuf", [128, 64], "int32"),
    "MK": ("sbuf", [128, 64], "float32"),
    "RS": ("sbuf", [128, 128], "float32"),
    "GM": ("sbuf", [128, 128], "float32"),
    "SC": ("sbuf", [128, 128], "float32"),
    "PI": ("sbuf", [128, 1], "int32"),
    "PA": ("sbuf", [128, 4], "int32"),
    "PF": ("sbuf", [128, 4], "float32"),
    "PG": ("sbuf", [128, 2], "float32"),
    "KB": ("sbuf", [128, 10], "float32"),
    "LST": ("sbuf", [128, 10], "uint16"),
    "VP": ("sbuf", [128, 160], "float32"),
    "VT": ("sbuf", [128, 160], "float32"),
    "OL": ("sbuf", [128, 5], "uint16"),
    "land": ("dram", [NR, 128, 5], "uint16"),
    "OFF": ("sbuf", [128, NR * 40], "uint16"),
    "R": ("sbuf", [128, NT * SLOT], "float32"),
    "Y": ("sbuf", [128, RD * NR * SH], "float32"),
}
for _b in range(8):
    SCRATCH["ps%d" % _b] = ("psum", [128, 512], "float32")

SEMAPHORES = ["ldw", "ldi", "ldd", "lde", "ldx", "ldy", "sv", "ss", "sp", "sg", "hwc", "hws", "hdc", "hds", "lsem", "own", "st"]
SEMAPHORES += ["aw%d" % _q for _q in range(NR)] + ["ad%d" % _q for _q in range(NR)]
SEMAPHORES += ["al%d" % _q for _q in range(NR)] + ["rp%d" % _q for _q in range(NR)]


def helper_table(T, topo, r):
    me = T.cores[r]
    cand = {}
    for h, (kind, jobs) in HELPERS.items():
        cand[h] = [c for c in topo.cores_of(me) if T.rank_of(c) is None
                   and (topo.die(c) == topo.die(me)) == (kind == "near")
                   and all(topo.may_write(c, T.cores[(r + k) % NR]) for _, ks in jobs for k in ks)]
    out = {}
    for h in sorted(cand, key=lambda e: len(cand[e])):
        free = [c for c in cand[h] if c not in out.values()]
        free.sort(key=lambda c: sum(1 for e in cand if c in cand[e]))
        out[h] = free[0]
    return out


def codes(T, a, b):
    return T.C[:, a:b].bitcast(dt.uint8)


def bits(engines):
    return sum(1 << e for e in engines)


def chip_engines(T, topo, r):
    me = T.cores[r]
    off = topo.engines(me, T.cores[(r + 1) % NR])
    return [e for e in topo.engines(me, list(helper_table(T, topo, r).values())[0]) if e not in off]


def view(T, r, what):
    a, b = PIECES[what[0]]
    if what[2:]:
        a, b = ((a, (a + b) // 2), ((a + b) // 2, b))[int(what[2])]
    return codes(T, SLOT * r + a, SLOT * r + b) if what[1] == "c" else T.CS[:, SLOT * r + a:SLOT * r + b]


def writes(piece, k):
    jobs = [(what, ks) for what, _, ks in CALLS] + [j for h in HELPERS for j in HELPERS[h][1]]
    return sum(1 for what, ks in jobs if what[0] == piece and k in ks)


def transfer(T, topo, cores, engines, out, src, sem):
    ids = [DstId(rid=topo.addr(c)[0], pnc=topo.addr(c)[1]) for c in cores]
    return RemoteDMATransfer(dst_ids=ids, dma_engine_mask=bits(engines), remote_sem=T.sem[sem], srcs=[src],
                             dsts=[out for c in cores])


def helper_program(g, core, T, topo):
    for r in range(NR):
        for h, c in helper_table(T, topo, r).items():
            if c != core:
                continue
            n = 0
            for what, ks in HELPERS[h][1]:
                cores = [T.cores[(r + k) % NR] for k in ks]
                engines = topo.engines(core, cores[0])
                g.wait_ge(T.sem["h" + what[0:2]], len(chip_engines(T, topo, r)))
                g.remote_dma_fused([transfer(T, topo, cores, engines, view(T, r, what), view(T, r, what),
                                             "a%s%d" % (what[0], r))], local_sem=T.sem.lsem)
                n += len(engines)
            g.wait_ge(T.sem.lsem, n)


def rank_program(g, core, T, topo):
    rank = T.rank_of(core)
    if rank is None:
        helper_program(g, core, T, topo)
        return
    add, mult = AluOpType.add, AluOpType.mult
    band, shr = AluOpType.bitwise_and, AluOpType.arith_shift_right
    Copy = ActivationFunctionType.Copy
    eng = {"g": g, "v": g.vector, "s": g.scalar, "p": g.tensor, "y": g.sync}
    cnt = {"sv": 0, "ss": 0, "sp": 0, "sg": 0}
    seen = {}

    def need(q, *toks):
        for t in toks:
            if t is not None and seen.get((q, t[0]), 0) < t[1]:
                eng[q].wait_ge(T.sem[t[0]], t[1])
                seen[(q, t[0])] = t[1]

    def tok(sem, ins):
        ins.then_inc(T.sem[sem], 1)
        cnt[sem] += 1
        return (sem, cnt[sem])

    V, S = g.vector, g.scalar
    dests = [(rank + k) % NR for k in range(1, NR)]
    base = SLOT * rank

    for k in range(2):
        e = g.scalar if k % 2 else g.sync
        e.dma_start(T.IDX[16 * k:16 * k + 16, :], T.idx[:]).then_inc(T.sem.ldi, 16)
    g.sync.dma_start(T.M[:, 0:4 * SH], T.wm[:]).then_inc(T.sem.ldw, 16)
    g.sync.dma_start(T.DL[:, 0:4 * CH], T.dl[:, 0:4 * CH]).then_inc(T.sem.ldd, 16)
    g.sync.dma_start(T.DL[:, 4 * CH:], T.dl[:, 4 * CH:]).then_inc(T.sem.lde, 16)
    if XE:
        g.sync.dma_start(T.XB[:, 0:512 * XE], T.x[:, 0:512 * XE]).then_inc(T.sem.ldy, 16)
    g.sync.dma_start(T.XB[:, 512 * XE:], T.x[:, 512 * XE:]).then_inc(T.sem.ldx, 16)
    w_w, w_i = ("ldw", 16), ("ldi", 32)

    t_pi = tok("sg", g.iota(T.PI[:], [[1, 1]], 0, 1))
    t_pt = tok("sg", g.iota(T.PT[:, 2 * SH:], [[1, SLOT]], 0, 0, allow_small_or_imprecise_dtypes=True))
    t_mi = tok("sg", g.iota(T.MI[:], [[0, 16], [1, 4]], 0, 0))
    t_kb = tok("sg", g.iota(T.KB[:], [[16, 5], [2, 2]], 0, 0, allow_small_or_imprecise_dtypes=True))
    t_r1 = tok("sv", V.memset(T.RS[:], 1.0))
    need("v", t_pi)
    V.tensor_scalar(T.PA[:, 0:1], T.PI[:], 7, None, band)
    V.tensor_scalar(T.PA[:, 1:2], T.PI[:], 3, None, shr)
    V.tensor_scalar(T.PA[:, 2:3], T.PI[:], 3, None, band)
    t_pa = tok("sv", V.tensor_scalar(T.PA[:, 3:4], T.PI[:], 2, 3, shr, band))
    need("v", t_r1)
    t_rs = tok("sv", V.memset(T.RS[:, 0:2 * CH:4], 0.0))
    need("v", t_pa)
    t_pf = tok("sv", V.tensor_copy(T.PF[:], T.PA[:]))
    need("v", t_pf)
    t_pg = tok("sv", V.tensor_scalar(T.PG[:, 0:1], T.PF[:, 0:1], 80.0, T.PF[:, 1:2], mult, add))

    def dq(k):
        need("s", ("lde" if k else "ldd", 16))
        return tok("ss", S.activation(T.DQ[:, 256 * k:256 * k + 256], T.DL[:, 256 * k:256 * k + 256], Copy, scale=0.25))

    def plane(t, *toks):
        need("v", *toks)
        a = 4 * SH
        return tok("sv", V.tensor_tensor(T.M[:, a + t:a + 4 * CH:4], T.M[:, t:a].indirect(T.I4[:]),
                                         T.DQ[:, t:256:4], add))

    def change(k, *toks):
        need("v", *toks)
        a = 4 * (SH + CH * k)
        return tok("sv", V.tensor_tensor(T.M[:, a:a + 4 * CH], T.M[:, 0:a].indirect(T.OF[:, 16 * k - 16:16 * k]),
                                         T.DQ[:, 256 * k:256 * k + 256], add))

    def table(t):
        return T.PT[:, SH * (3 - t):SH * (4 - t)]

    def scatter(k, *toks):
        need("v", *toks)
        a = 3 * SH + CH * k
        return tok("sv", V.tensor_copy(table(k + 1).indirect(T.I16[:, 4 * k:4 * k + 4]), T.PT[:, a:a + CH]))

    def seg(k, *toks):
        need("s", *toks)
        return tok("ss", S.activation(table(k + 1), table(k), Copy))

    def look(k, *toks):
        need("v", *toks)
        return tok("sv", V.tensor_tensor(T.GM[:, CH * k - CH:CH * k],
                                         table(k).indirect(T.I16[:, 4 * k:4 * k + 4]), T.MK[:], mult))

    t_qx = {}

    def quant_x(a, b):
        if a < b:
            need("v", ("ldx" if b > XE else "ldy", 16))
            z = tok("sv", V.quantize_mx(T.XC[:, 128 * a:128 * b], T.XS[:, 128 * a:128 * b], T.XB[:, 512 * a:512 * b]))
            t_qx.update({t: z for t in range(a, b)})

    def quant(a, b, *toks):
        need("v", *toks)
        return tok("sv", V.quantize_mx(T.C[:, base + a:base + b], T.CS[:, base + a:base + b], T.M[:, 4 * a:4 * b]))

    def on(q, toks, call):
        need(q, *toks)
        return tok("s" + q, call())

    def narrow():
        need("v", w_i)
        for k in range(0, 96, 32):
            V.tensor_copy(T.I16[k:k + 32, :], T.IDX[0:32, :])
        return tok("sv", V.tensor_copy(T.I16[96:128, :], T.IDX[0:32, :]))

    z = {}
    steps = {
        "q0": lambda: quant(0, SH, w_w),
        "i16": narrow,
        "mk": lambda: on("v", [t_pf, t_mi],
                         lambda: V.tensor_scalar(T.MK[:], T.MI[:], T.PF[:, 3:4], 4.0, AluOpType.is_equal, mult)),
        "ls": lambda: on("v", [t_pg, t_kb], lambda: V.tensor_scalar(T.LST[:], T.KB[:], T.PG[:, 0:1], None, add)),
        "i4": lambda: on("v", [z["i16"]], lambda: V.tensor_scalar(T.I4[:], T.I16[:, 0:4], 4, None, mult)),
        "dq1": lambda: dq(0), "dq2": lambda: dq(1), "dq3": lambda: dq(2),
        "sc1": lambda: scatter(0, z["i16"], t_pt),
        "sc2": lambda: scatter(1, z["seg2"]),
        "sc3": lambda: scatter(2, z["seg3"]),
        "seg2": lambda: seg(1, z["sc1"]),
        "seg3": lambda: seg(2, z["sc2"]),
        "look2": lambda: look(1, z["sc1"], z["mk"]),
        "look3": lambda: look(2, z["sc2"], z["mk"]),
        "p0": lambda: plane(0, z["i4"], z["dq1"], w_w),
        "p1": lambda: plane(1), "p2": lambda: plane(2), "p3": lambda: plane(3),
        "scan": lambda: on("v", [z["look2"], z["look3"], t_rs],
                           lambda: V.tensor_tensor_scan(T.SC[:], T.RS[:], T.GM[:], 0.0, mult, add)),
        "of": lambda: on("v", [z["scan"]],
                         lambda: V.tensor_scalar(T.OF[:], T.SC[:, 3:2 * CH:4], T.PF[:, 2:3], None, add)),
        "d2": lambda: change(1, z["of"], z["dq2"], z["p3"]),
        "d3": lambda: change(2, z["dq3"], z["d2"]),
        "vp": lambda: on("s", [z["sc3"], z["ls"]],
                         lambda: S.activation(T.VP[:], T.PT[:].indirect(T.LST[:]), Copy)),
        "vt": lambda: on("v", [z["vp"]], lambda: V.transpose(T.VT[:], T.VP[:])),
        "ol": lambda: on("v", [z["vt"]], lambda: V.tensor_copy(T.OL[:], T.VT[:, 0:160:32])),
        "qd": lambda: quant(SH, SLOT, z["d3"]),
        "xa": lambda: quant_x(0, XE), "xb": lambda: quant_x(XE, RD),
    }
    for name in CHAIN.split():
        z[name] = steps[name]()
    t_q0, t_qd, t_ol = z["q0"], z["qd"], z["ol"]

    nl = [0]
    ht = helper_table(T, topo, rank)

    off_chip = topo.engines(core, T.cores[dests[0]])
    on_chip = chip_engines(T, topo, rank)
    made = {"w": t_q0, "d": t_qd, "l": t_ol}
    for what, hs, ks in CALLS:
        need("g", made[what[0]])
        if GATE and (what, hs, ks) == CALLS[-1]:
            need("g", ("own", 1))
        trs = []
        if what == "lists":
            trs.append(transfer(T, topo, [T.cores[d] for d in dests], off_chip, T.land[rank], T.OL[:], "al%d" % rank))
        if hs:
            v = view(T, rank, what)
            trs.append(transfer(T, topo, [ht[h] for h in hs], on_chip, v, v, "h" + what[0:2]))
        if ks:
            v = view(T, rank, what)
            trs.append(transfer(T, topo, [T.cores[(rank + k) % NR] for k in ks], off_chip, v, v,
                                "a%s%d" % (what[0], rank)))
        g.remote_dma_fused(trs, local_sem=T.sem.lsem)
        nl[0] += len(on_chip) * bool(hs) + len(off_chip) * (len(trs) - bool(hs))

    order = [(rank - k) % NR for k in range(1, NR)]

    def spread(q):
        need("y", t_ol if q == rank else ("al%d" % q, len(off_chip)))
        src, a = T.OL[:] if q == rank else T.land[q], 40 * ((rank - q) % NR)
        n = NSP[q != rank]
        for k in range(n):
            g.sync.dma_start(T.OFF[16 * k:16 * k + 16, a:a + 40], src).then_inc(T.sem["rp%d" % q], 16)
        tables[q] = ("rp%d" % q, 16 * n)
        if GATE and len(tables) == NR:
            g.sync.sem_inc(T.sem.own, 1)

    tables = {}

    def repeat(*qs):
        need("v", *[tables[q] for q in qs])
        a, b = 40 * ((rank - qs[0]) % NR), 40 * ((rank - qs[-1]) % NR + 1)
        n = 16 * NSP[qs[0] != rank]
        for k in range(n, 128, n):
            z = tok("sv", V.tensor_copy(T.OFF[k:k + n, a:b], T.OFF[0:n, a:b]))
            tables.update({q: z for q in qs})

    banks, held, nst = [], {}, [0]

    def product(q, t, parts, e):
        a = 0 if "w" in parts else SH
        n = (SH + CH * t if "d" in parts else SH) - a
        j = len(banks)
        bank = T["ps%d" % (j % 8)]
        need("p", t_qx[t], *[made[p] if q == rank else ("a%s%d" % (p, q), writes(p, (rank - q) % NR) * len(off_chip))
                             for p in parts])
        if j >= 8:
            need("p", banks[j - 8])
        c, w = SLOT * q + a, max(n, 128)
        mm = tok("sp", g.tensor.matmul_mx(bank[:, 0:w], T.XC[:, 128 * t:128 * t + 128], T.XS[:, 128 * t:128 * t + 128],
                                          T.C[:, c:c + w], T.CS[:, c:c + w], True, True))
        o = SLOT * (3 * q + t - 1) + a
        out = T.R[:, o:o + n] if t else T.Y[:, SH * q:SH * q + SH]
        need(e, mm)
        z = tok("ss", S.activation(out, bank[:, 0:n], Copy)) if e == "s" else tok("sv", V.tensor_copy(out, bank[:, 0:n]))
        banks.append(z)
        held.setdefault((q, t), []).append(z)

    ready = {}

    def store(q, t, z):
        ready[t * NR + q] = z

    def flush():
        while ready:
            a = b = min(ready)
            while b in ready:
                need("y", ready.pop(b))
                b += 1
            g.sync.dma_start(T.y[:, SH * a:SH * b], T.Y[:, SH * a:SH * b]).then_inc(T.sem.st, 16)
            nst[0] += 16

    def pick(q, t, e):
        need(e, tables[q], *held[q, t])
        o, k, blk = SLOT * (3 * q + t - 1), 40 * ((rank - q) % NR) + 10 * (3 - t), SH * (t * NR + q)
        win = T.R[:, o:o + SH + CH * t].indirect(T.OFF[:, k:k + 10])
        out = T.Y[:, blk:blk + SH]
        store(q, t, tok("ss", S.activation(out, win, Copy)) if e == "s" else tok("sv", V.tensor_copy(out, win)))

    def early(q, ts=(1, 3, 2, 0), e=None):
        for t in ts:
            product(q, t, "w", e or QUEUE[t])
            if t == 0:
                store(q, 0, held[q, 0][0])

    def late(q, ts=(1, 3, 2), e=None):
        for t in ts:
            product(q, t, "wd" if (q, t) not in held else "d", e or QUEUE[t])

    def picks(*qs):
        for t in (1, 3, 2):
            for q in qs:
                pick(q, t, QUEUE[t])
            flush()

    first, second, far = order
    spread(rank)
    for q in order:
        spread(q)
    early(rank, [0])
    flush()
    late(rank)
    repeat(rank)
    early(first)
    picks(rank)
    early(second)
    early(far)
    flush()
    repeat(*order)
    late(first)
    picks(first)
    late(second)
    picks(second)
    late(far)
    picks(far)

    need("y", ("st", nst[0]))
    for s in ("sg", "sv", "ss", "sp"):
        need("y", (s, cnt[s]))
    need("g", ("lsem", nl[0]))
